import numpy as np
import ml_dtypes


def mxq(x, axis, fmt="e4m3"):
    dtype, down = {"e4m3": (ml_dtypes.float8_e4m3fn, 7), "e5m2": (ml_dtypes.float8_e5m2, 14)}[fmt]
    v = np.moveaxis(np.asarray(x, np.float32).astype(ml_dtypes.bfloat16).astype(np.float64), axis, -1)
    blocks = v.reshape(v.shape[:-1] + (-1, 32))
    amax = np.abs(blocks).max(-1, keepdims=True)
    byte = np.maximum(np.where(amax > 0, np.frexp(amax)[1] - 1 + 127, 0) - down, 1)
    scale = np.exp2(byte - 127.0)
    codes = (blocks / scale).astype(np.float32).astype(dtype).astype(np.float64)
    return np.moveaxis((codes * scale).reshape(v.shape), -1, axis)


WIDE = False


def mx_kscale(k):
    if not WIDE:
        return np.ones(k)
    levels = np.array([10, -10, 5, -5, 0])
    if k % 512:
        return np.exp2(np.random.permutation(np.resize(levels, k // 32))).repeat(32)
    a = np.empty((k // 512, 16))
    for p in range(k // 512):
        a[p, :8] = np.random.permutation(np.resize(levels, 8))
        for g in range(8):
            far = levels[np.abs(levels - a[p, g]) >= 10]
            a[p, g + 8] = far[np.random.randint(len(far))]
    return np.exp2(a.ravel()).repeat(32)


def f64(x):
    return np.asarray(x).astype(np.float64)


def striped(idx):
    return np.tile(idx.reshape(-1, 16).T, (8, 1)).astype(np.uint16)


def unstriped(offs):
    return offs[:16].T.reshape(-1).astype(np.int64)


E2M1 = np.array([0.0, 0.5, 1.0, 1.5, 2.0, 3.0, 4.0, 6.0, -0.0, -0.5, -1.0, -1.5, -2.0, -3.0, -4.0, -6.0])


def pack_weight(w, fmt):
    k, n = w.shape
    w = f64(np.asarray(w, np.float32).astype(ml_dtypes.bfloat16)).reshape(k // 32, 32, n)
    amax = np.abs(w).max(1)
    if fmt == "e4m3":
        byte = np.frexp(amax)[1] - 1 + 127 - 7
    else:
        mant, ex = np.frexp(amax / 6.0)
        byte = np.where(mant > 0.5, ex, ex - 1) + 127
    byte = np.clip(np.where(amax > 0, byte, 1), 1, 254)
    scaled = (w * np.exp2(127.0 - byte)[:, None, :]).reshape(k, n).astype(np.float32)
    by_word = np.ascontiguousarray(scaled.reshape(k // 512, 128, 4, n).transpose(0, 1, 3, 2))
    if fmt == "e4m3":
        words = by_word.astype(ml_dtypes.float8_e4m3fn).view(np.uint8)
    else:
        c = by_word.astype(ml_dtypes.float4_e2m1fn).view(np.uint8) & 0xF
        words = (c[..., 0::2] | (c[..., 1::2] << 4)).reshape(k // 512, 128, 2 * n)
    return np.ascontiguousarray(words), np.ascontiguousarray(byte.astype(np.uint8).reshape(k // 512, 16, n))


def unpack_weight(words, scales, fmt):
    g, _, n = scales.shape
    words = np.ascontiguousarray(words).reshape(g, 128, n, -1)
    if fmt == "e4m3":
        vals = words.view(ml_dtypes.float8_e4m3fn).astype(np.float64)
    else:
        nib = np.empty((g, 128, n, 4), np.uint8)
        nib[..., 0::2] = words & 0xF
        nib[..., 1::2] = words >> 4
        vals = E2M1[nib]
    vals = vals * np.repeat(np.exp2(scales.astype(np.float64) - 127.0), 8, axis=1)[..., None]
    return vals.transpose(0, 1, 3, 2).reshape(g * 512, n)


def gelu(v):
    return 0.5 * v * (1.0 + np.tanh(np.sqrt(2.0 / np.pi) * (v + 0.044715 * v**3)))


K, H, T, S, T3, S2, P = 1024, 512, 2048, 1024, 4096, 1024, 512

def setup_inputs():
    n = np.random.standard_normal
    s = mx_kscale(K)[:, None]
    u = mx_kscale(H)[:, None]
    d = {}
    d["tab_words"], d["tab_scales"] = pack_weight(n((K, T)) * s, "e4m3")
    d["tab2_words"], d["tab2_scales"] = pack_weight(n((H, T3)) / H**0.5 / u, "e4m3")
    d["offs"] = striped(np.random.permutation(T)[:S])
    d["offs2"] = striped(np.random.permutation(T3)[:S2])
    d["pos1"] = striped(np.random.permutation(S)[:P])
    d["pos2"] = striped(np.random.permutation(S)[:P])
    d["w1"] = (2.0 * n((K, H)) / K**0.5 / s * u.T).astype(np.float32)
    d["wg_words"], d["wg_scales"] = pack_weight(2.0 * n((K, H)) / K**0.5 / s, "e2m1")
    d["bg"] = (0.7 * n(H)).astype(np.float32)
    d["cut"] = np.random.uniform(0.1, 0.5, H).astype(np.float32)
    d["cap1"] = np.exp(0.4 * n(S2)).astype(np.float32)
    d["cap2"] = np.exp(0.4 * n(S2)).astype(np.float32)
    return d

def reference(tab_words, tab_scales, tab2_words, tab2_scales, offs, offs2, pos1, pos2,
              w1, wg_words, wg_scales, bg, cut, cap1, cap2):
    v = unpack_weight(tab_words, tab_scales, "e4m3")[:, unstriped(offs)]
    v2 = unpack_weight(tab2_words, tab2_scales, "e4m3")[:, unstriped(offs2)]
    wg = unpack_weight(wg_words, wg_scales, "e2m1")
    need = mxq(f64(w1), 0, "e4m3").T @ v
    urge = 1.0 / (1.0 + np.exp(-((wg.T @ v) + f64(bg)[:, None])))
    h = need * (urge - f64(cut)[:, None])
    e = v2.T @ mxq(h, 0, "e4m3")
    e1 = e[:, unstriped(pos1)] * f64(cap1)[:, None]
    e2 = e[:, unstriped(pos2)] * f64(cap2)[:, None]
    return np.minimum(e1, e2)

@@ -1,0 +1,254 @@
+from contextlib import ExitStack
+
+import concourse.mybir as mybir
+
+K, H, T, S, T3, S2, NP = 1024, 512, 2048, 1024, 4096, 1024, 512
+FLOPS = 2 * (2 * K * H * S + H * S2 * S)
+
+F32 = mybir.dt.float32
+BF16 = mybir.dt.bfloat16
+I32 = mybir.dt.int32
+U32 = mybir.dt.uint32
+U16 = mybir.dt.uint16
+U8 = mybir.dt.uint8
+FP8X4 = mybir.dt.float8_e4m3fn_x4
+FP4X4 = mybir.dt.float4_e2m1fn_x4
+ALU = mybir.AluOpType
+ACT = mybir.ActivationFunctionType
+
+P = 128
+PACK = 4
+PASSES = K // (P * PACK)
+BANK = 512
+HALVES = S // BANK
+QUADS = 4
+M_TILES = S2 // P
+LIST_COLS = BANK // 16
+
+
+def tile_list_sibling_placement_scores_kernel(
+    tc, tab_words, tab_scales, tab2_words, tab2_scales, offs, offs2, pos1, pos2,
+    w1, wg_words, wg_scales, bg, cut, cap1, cap2, out,
+):
+    nc = tc.nc
+    with ExitStack() as ctx:
+        lists = ctx.enter_context(tc.tile_pool(name="lists", bufs=1))
+        keep = ctx.enter_context(tc.tile_pool(name="keep", bufs=1))
+        ring = ctx.enter_context(tc.tile_pool(name="ring", bufs=3))
+        psum = ctx.enter_context(tc.psum_pool(name="psum", bufs=1))
+
+        def held(name, shape, dtype):
+            return keep.tile(shape, dtype, name=name, align_bytes=64)
+
+        def load_list(name, src):
+            tile = lists.tile(list(src.shape), U16, name=name)
+            nc.sync.dma_start(tile[:], src)
+            return tile
+
+        def load_words(name, src):
+            tile = held(name, [P, src.shape[1]], I32)
+            nc.sync.dma_start(tile[:], src.rearrange("p t i -> p (t i)").bitcast(I32))
+            return tile
+
+        def load_w1(name, a, c0, c1):
+            tile = held(name, [P, PACK, c1 - c0], F32)
+            rows = w1[a * P * PACK : (a + 1) * P * PACK, c0:c1]
+            nc.sync.dma_start(tile[:], rows.rearrange("(p j) c -> p j c", j=PACK))
+            return tile
+
+        def bank(b):
+            return psum.tile([P, BANK], F32, name="bank%d" % b)
+
+        tab_plane = held("tab_plane", [P, T], U8)
+        wg_plane = held("wg_plane", [P, PASSES * H], U8)
+        tab2_plane = held("tab2_plane", [P, T3], U8)
+        v_scale1 = held("v_scale1", [P, S], U8)
+        for plane in (tab_plane, wg_plane, tab2_plane, v_scale1):
+            nc.vector.memset(plane[:].bitcast(I32), 0)
+
+        warm = held("warm", [P, 2], F32)
+        nc.vector.memset(warm[:, 0:1], 0.0)
+
+        offs_t = load_list("offs_t", offs)
+        wg_raw = held("wg_raw", [P, PASSES, 2 * H // 4], I32)
+        nc.sync.dma_start(wg_raw[:], wg_words.bitcast(I32).rearrange("a p n -> p a n"))
+        bg_t = held("bg_t", [P, PACK], F32)
+        cut_t = held("cut_t", [P, PACK], F32)
+        nc.sync.dma_start(bg_t[:], bg.rearrange("(p t) -> p t", t=PACK))
+        nc.sync.dma_start(cut_t[:], cut.rearrange("(p t) -> p t", t=PACK))
+        for q in range(QUADS):
+            nc.scalar.dma_start(
+                tab_plane[32 * q : 32 * q + 4 * PASSES, :].bitcast(I32),
+                tab_scales[:, 4 * q : 4 * q + 4, :].bitcast(I32),
+            )
+        nc.scalar.activation(warm[:, 1:2], warm[:, 0:1], ACT.Sigmoid)
+        w1_raw0 = load_w1("w1_raw0", 0, 0, H)
+        tab_w0 = load_words("tab_w0", tab_words[0])
+        offs2_t = load_list("offs2_t", offs2)
+        tab_w1 = load_words("tab_w1", tab_words[1])
+        w1_raw1 = [load_w1("w1_raw1%d" % c, 1, c * H // 2, (c + 1) * H // 2) for c in range(2)]
+        for q in range(QUADS):
+            nc.sync.dma_start(
+                tab2_plane[32 * q : 32 * q + 4, :].bitcast(I32),
+                tab2_scales[0, 4 * q : 4 * q + 4, :].bitcast(I32),
+            )
+        tab2_w = load_words("tab2_w", tab2_words[0])
+        pos1_t = load_list("pos1_t", pos1)
+        pos2_t = load_list("pos2_t", pos2)
+        cap1_t = held("cap1_t", [P, M_TILES], F32)
+        cap2_t = held("cap2_t", [P, M_TILES], F32)
+        with nc.allow_non_contiguous_dma(reason="one capacity a partition and tile"):
+            nc.sync.dma_start(cap1_t[:], cap1.rearrange("(i p) -> p i", p=P))
+            nc.sync.dma_start(cap2_t[:], cap2.rearrange("(i p) -> p i", p=P))
+
+        for q in range(QUADS):
+            nc.gpsimd.dma_start(
+                wg_plane[32 * q : 32 * q + 4, :].bitcast(I32).rearrange("r (a n) -> r a n", a=PASSES),
+                wg_scales[:, 4 * q : 4 * q + 4, :].bitcast(I32).rearrange("a r n -> r a n"),
+            )
+
+        v_scale0 = held("v_scale0", [P, S], U8)
+        nc.vector.tensor_copy(v_scale0[:], tab_plane[:].indirect(offs_t[:]))
+        nc.gpsimd.dma_start(v_scale1[0:112, :].bitcast(I32), v_scale0[4:116, :].bitcast(I32))
+        v_scale = [v_scale0, v_scale1]
+
+
+        wg_codes = held("wg_codes", [P, PASSES * 2 * H], U8)
+        wg_sc = held("wg_sc", [P, PASSES * H], U8)
+        nc.vector.tensor_copy(
+            wg_codes[:].bitcast(U16).rearrange("p (a t m) -> p a m t", a=PASSES, t=PACK),
+            wg_raw[:].rearrange("p a n -> p (a n)").bitcast(U16).rearrange("p (a m t) -> p a m t", a=PASSES, t=PACK),
+        )
+        nc.vector.tensor_copy(
+            wg_sc[:].rearrange("p (a t m) -> p a m t", a=PASSES, t=PACK),
+            wg_plane[:].rearrange("p (a m t) -> p a m t", a=PASSES, t=PACK),
+        )
+
+        w1_bf = [held("w1_bf%d" % a, [P, H * PACK], BF16) for a in range(PASSES)]
+        w1_codes = [held("w1_codes%d" % a, [P, H], U32) for a in range(PASSES)]
+        w1_sc = [held("w1_sc%d" % a, [P, H], U8) for a in range(PASSES)]
+
+        def round_w1(a, raw, c0):
+            m0, m1 = c0 // PACK, (c0 + raw.shape[2]) // PACK
+            dealt = w1_bf[a][:].rearrange("p (t m j) -> p m j t", t=PACK, j=PACK)
+            nc.scalar.copy(dealt[:, m0:m1, :, :], raw[:].rearrange("p j (m t) -> p m j t", t=PACK))
+
+        def quantize(codes, scales, values):
+            nc.vector.quantize_mx(out=codes.bitcast(FP8X4), scales=scales, in_=values)
+
+        def gather_words(name, table, offsets, h):
+            tile = held(name, [P, BANK], U32)
+            picked = table[:].bitcast(U32).indirect(offsets[:, h * LIST_COLS : (h + 1) * LIST_COLS])
+            nc.vector.tensor_copy(tile[:], picked)
+            return tile
+
+        round_w1(0, w1_raw0, 0)
+        v_words = [[None] * HALVES for a in range(PASSES)]
+        for h in range(HALVES):
+            v_words[0][h] = gather_words("v_words0%d" % h, tab_w0, offs_t, h)
+        quantize(w1_codes[0][:], w1_sc[0][:], w1_bf[0][:])
+        for h in range(HALVES):
+            v_words[1][h] = gather_words("v_words1%d" % h, tab_w1, offs_t, h)
+
+        def pass_need(acc, t, h, a):
+            cols = slice(t * P, (t + 1) * P)
+            nc.tensor.matmul_mx(
+                out=acc[:], lhsT=w1_codes[a][:, cols].bitcast(FP8X4), lhsT_scale=w1_sc[a][:, cols],
+                rhs=v_words[a][h][:].bitcast(FP8X4), rhs_scale=v_scale[a][:, h * BANK : (h + 1) * BANK],
+                start=(a == 0), stop=(a == PASSES - 1),
+            )
+
+        def pass_gate(acc, t, h, a):
+            c0 = a * H + t * P
+            nc.tensor.matmul_mx(
+                out=acc[:], lhsT=wg_codes[:, 2 * c0 : 2 * (c0 + P)].bitcast(FP4X4), lhsT_scale=wg_sc[:, c0 : c0 + P],
+                rhs=v_words[a][h][:].bitcast(FP8X4), rhs_scale=v_scale[a][:, h * BANK : (h + 1) * BANK],
+                start=(a == 0), stop=(a == PASSES - 1),
+            )
+
+        urge = [[held("urge%d%d" % (h, t), [P, BANK], F32) for t in range(PACK)] for h in range(HALVES)]
+        h_rows = [held("h_rows%d" % h, [P, PACK, BANK], BF16) for h in range(HALVES)]
+        h_woven = [held("h_woven%d" % h, [P, BANK * PACK], BF16) for h in range(HALVES)]
+        h_codes = [held("h_codes%d" % h, [P, BANK], U32) for h in range(HALVES)]
+        h_sc = [held("h_sc%d" % h, [P, BANK], U8) for h in range(HALVES)]
+
+        def sigmoid(acc, t, h):
+            nc.scalar.activation(urge[h][t][:], acc[:], ACT.Sigmoid, bias=bg_t[:, t : t + 1])
+
+        def product(acc, t, h):
+            nc.vector.scalar_tensor_tensor(
+                h_rows[h][:, t, :], urge[h][t][:], cut_t[:, t : t + 1], acc[:], ALU.subtract, ALU.mult
+            )
+
+        def weave(copy, h):
+            copy(
+                h_woven[h][:].rearrange("p (c i t) -> p c t i", i=PACK, t=PACK),
+                h_rows[h][:].rearrange("p t (c i) -> p c t i", i=PACK),
+            )
+
+        gate0 = [bank(t) for t in range(PACK)]
+        need0 = [bank(PACK + t) for t in range(PACK)]
+        for t in range(PACK):
+            pass_gate(gate0[t], t, 0, 0)
+        for t in range(PACK):
+            pass_need(need0[t], t, 0, 0)
+        round_w1(1, w1_raw1[0], 0)
+        for t in range(PACK):
+            pass_gate(gate0[t], t, 0, 1)
+        sigmoid(gate0[0], 0, 0)
+        round_w1(1, w1_raw1[1], H // 2)
+        for t in range(1, PACK):
+            sigmoid(gate0[t], t, 0)
+
+        v2_scale = held("v2_scale", [P, S2], U8)
+        nc.vector.tensor_copy(v2_scale[:], tab2_plane[:].indirect(offs2_t[:]))
+
+        for half in range(2):
+            cols = slice(half * H // 2, (half + 1) * H // 2)
+            quantize(w1_codes[1][:, cols], w1_sc[1][:, cols], w1_bf[1][:, half * 2 * H : (half + 1) * 2 * H])
+        for t in range(PACK):
+            pass_need(need0[t], t, 0, 1)
+        gate1 = [bank(t) for t in range(PACK)]
+        for t in range(PACK):
+            for a in range(PASSES):
+                pass_gate(gate1[t], t, 1, a)
+        for t in range(PACK):
+            product(need0[t], t, 0)
+        for t in range(PACK):
+            sigmoid(gate1[t], t, 1)
+        need1 = [bank(PACK + t) for t in range(PACK)]
+        for t in range(PACK):
+            for a in range(PASSES):
+                pass_need(need1[t], t, 1, a)
+        weave(nc.scalar.copy, 0)
+        for t in range(PACK):
+            product(need1[t], t, 1)
+        v2_words = [gather_words("v2_words0", tab2_w, offs2_t, 0)]
+        weave(nc.vector.tensor_copy, 1)
+        for h in range(HALVES):
+            quantize(h_codes[h][:], h_sc[h][:], h_woven[h][:])
+        v2_words.append(gather_words("v2_words1", tab2_w, offs2_t, 1))
+
+        tiles_a_slice = BANK // P
+        for i in range(M_TILES):
+            c0 = (i % tiles_a_slice) * P
+            scores = ring.tile([P, S], F32, name="scores")
+            for h in range(HALVES):
+                acc = bank((HALVES * i + h) % 8)
+                nc.tensor.matmul_mx(
+                    out=acc[:], lhsT=v2_words[i // tiles_a_slice][:, c0 : c0 + P].bitcast(FP8X4),
+                    lhsT_scale=v2_scale[:, i * P : (i + 1) * P],
+                    rhs=h_codes[h][:].bitcast(FP8X4), rhs_scale=h_sc[h][:], start=True, stop=True,
+                )
+                nc.scalar.copy(scores[:, h * BANK : (h + 1) * BANK], acc[:])
+            first = ring.tile([P, NP], F32, name="first")
+            second = ring.tile([P, NP], F32, name="second")
+            first_cap = ring.tile([P, NP], F32, name="first_cap")
+            lower = ring.tile([P, NP], F32, name="lower")
+            nc.vector.tensor_copy(first[:], scores[:].indirect(pos1_t[:]))
+            nc.vector.tensor_copy(second[:], scores[:].indirect(pos2_t[:]))
+            nc.scalar.activation(first_cap[:], first[:], ACT.Copy, scale=cap1_t[:, i : i + 1])
+            nc.vector.scalar_tensor_tensor(
+                lower[:], second[:], cap2_t[:, i : i + 1], first_cap[:], ALU.mult, ALU.min
+            )
+            nc.sync.dma_start(out[i * P : (i + 1) * P, :], lower[:])

@@ -37,8 +37,8 @@ def tile_list_sibling_placement_scores_kernel(
         ring = ctx.enter_context(tc.tile_pool(name="ring", bufs=3))
         psum = ctx.enter_context(tc.psum_pool(name="psum", bufs=1))
 
-        def held(name, shape, dtype):
-            return keep.tile(shape, dtype, name=name, align_bytes=64)
+        def held(name, shape, dtype, tag=None):
+            return keep.tile(shape, dtype, name=name, tag=tag or name, align_bytes=64)
 
         def load_list(name, src):
             tile = lists.tile(list(src.shape), U16, name=name)
@@ -63,35 +63,43 @@ def tile_list_sibling_placement_scores_kernel(
         wg_plane = held("wg_plane", [P, PASSES * H], U8)
         tab2_plane = held("tab2_plane", [P, T3], U8)
         v_scale1 = held("v_scale1", [P, S], U8)
-        for plane in (tab_plane, wg_plane, tab2_plane, v_scale1):
+        v2_scale = [held("v2_scale%d" % h, [P, BANK], U8) for h in range(HALVES)]
+        for plane in (tab_plane, wg_plane, tab2_plane, v_scale1, *v2_scale):
             nc.vector.memset(plane[:].bitcast(I32), 0)
+
 
         warm = held("warm", [P, 2], F32)
         nc.vector.memset(warm[:, 0:1], 0.0)
+        nc.scalar.activation(warm[:, 1:2], warm[:, 0:1], ACT.Sigmoid)
 
         offs_t = load_list("offs_t", offs)
+        for r in range(4):
+            nc.sync.dma_start(
+                tab_plane[r : P : 16, :].bitcast(I32),
+                tab_scales[:, r : 16 : 4, :].bitcast(I32).rearrange("a q n -> q a n"),
+            )
         wg_raw = held("wg_raw", [P, PASSES, 2 * H // 4], I32)
         nc.sync.dma_start(wg_raw[:], wg_words.bitcast(I32).rearrange("a p n -> p a n"))
+        tab_w0 = load_words("tab_w0", tab_words[0])
+        for r in range(4):
+            nc.sync.dma_start(
+                wg_plane[r : P : 32, :].bitcast(I32).rearrange("q (a n) -> q a n", a=PASSES),
+                wg_scales[:, r : 16 : 4, :].bitcast(I32).rearrange("a q n -> q a n"),
+            )
+        offs2_t = load_list("offs2_t", offs2)
+        nc.sync.dma_start(tab2_plane[0 : P : 8, :].bitcast(I32), tab2_scales[0].bitcast(I32))
+        w1_raw0 = load_w1("w1_raw0", 0, 0, H)
+        tab_w1 = load_words("tab_w1", tab_words[1])
+
+        v_scale0 = held("v_scale0", [P, S], U8)
+        nc.vector.tensor_copy(v_scale0[:], tab_plane[:].indirect(offs_t[:]))
+        nc.sync.dma_start(v_scale1[0:112, :].bitcast(I32), v_scale0[16:128, :].bitcast(I32))
+        v_scale = [v_scale0, v_scale1]
         bg_t = held("bg_t", [P, PACK], F32)
         cut_t = held("cut_t", [P, PACK], F32)
+        w1_raw1 = [load_w1("w1_raw1%d" % c, 1, c * H // 2, (c + 1) * H // 2) for c in range(2)]
         nc.sync.dma_start(bg_t[:], bg.rearrange("(p t) -> p t", t=PACK))
         nc.sync.dma_start(cut_t[:], cut.rearrange("(p t) -> p t", t=PACK))
-        for q in range(QUADS):
-            nc.scalar.dma_start(
-                tab_plane[32 * q : 32 * q + 4 * PASSES, :].bitcast(I32),
-                tab_scales[:, 4 * q : 4 * q + 4, :].bitcast(I32),
-            )
-        nc.scalar.activation(warm[:, 1:2], warm[:, 0:1], ACT.Sigmoid)
-        w1_raw0 = load_w1("w1_raw0", 0, 0, H)
-        tab_w0 = load_words("tab_w0", tab_words[0])
-        offs2_t = load_list("offs2_t", offs2)
-        tab_w1 = load_words("tab_w1", tab_words[1])
-        w1_raw1 = [load_w1("w1_raw1%d" % c, 1, c * H // 2, (c + 1) * H // 2) for c in range(2)]
-        for q in range(QUADS):
-            nc.sync.dma_start(
-                tab2_plane[32 * q : 32 * q + 4, :].bitcast(I32),
-                tab2_scales[0, 4 * q : 4 * q + 4, :].bitcast(I32),
-            )
         tab2_w = load_words("tab2_w", tab2_words[0])
         pos1_t = load_list("pos1_t", pos1)
         pos2_t = load_list("pos2_t", pos2)
@@ -101,54 +109,49 @@ def tile_list_sibling_placement_scores_kernel(
             nc.sync.dma_start(cap1_t[:], cap1.rearrange("(i p) -> p i", p=P))
             nc.sync.dma_start(cap2_t[:], cap2.rearrange("(i p) -> p i", p=P))
 
-        for q in range(QUADS):
-            nc.gpsimd.dma_start(
-                wg_plane[32 * q : 32 * q + 4, :].bitcast(I32).rearrange("r (a n) -> r a n", a=PASSES),
-                wg_scales[:, 4 * q : 4 * q + 4, :].bitcast(I32).rearrange("a r n -> r a n"),
-            )
-
-        v_scale0 = held("v_scale0", [P, S], U8)
-        nc.vector.tensor_copy(v_scale0[:], tab_plane[:].indirect(offs_t[:]))
-        nc.gpsimd.dma_start(v_scale1[0:112, :].bitcast(I32), v_scale0[4:116, :].bitcast(I32))
-        v_scale = [v_scale0, v_scale1]
-
-
         wg_codes = held("wg_codes", [P, PASSES * 2 * H], U8)
         wg_sc = held("wg_sc", [P, PASSES * H], U8)
         nc.vector.tensor_copy(
-            wg_codes[:].bitcast(U16).rearrange("p (a t m) -> p a m t", a=PASSES, t=PACK),
-            wg_raw[:].rearrange("p a n -> p (a n)").bitcast(U16).rearrange("p (a m t) -> p a m t", a=PASSES, t=PACK),
+            wg_codes[:].bitcast(U16).rearrange("p (a t m) -> p a t m", a=PASSES, t=PACK),
+            wg_raw[:].rearrange("p a n -> p (a n)").bitcast(U16).rearrange("p (a m t) -> p a t m", a=PASSES, t=PACK),
         )
         nc.vector.tensor_copy(
-            wg_sc[:].rearrange("p (a t m) -> p a m t", a=PASSES, t=PACK),
-            wg_plane[:].rearrange("p (a m t) -> p a m t", a=PASSES, t=PACK),
+            wg_sc[:].rearrange("p (a t m) -> p a t m", a=PASSES, t=PACK),
+            wg_plane[:].rearrange("p (a m t) -> p a t m", a=PASSES, t=PACK),
         )
 
         w1_bf = [held("w1_bf%d" % a, [P, H * PACK], BF16) for a in range(PASSES)]
         w1_codes = [held("w1_codes%d" % a, [P, H], U32) for a in range(PASSES)]
         w1_sc = [held("w1_sc%d" % a, [P, H], U8) for a in range(PASSES)]
 
-        def round_w1(a, raw, c0):
+        def round_w1(copy, a, raw, c0):
             m0, m1 = c0 // PACK, (c0 + raw.shape[2]) // PACK
             dealt = w1_bf[a][:].rearrange("p (t m j) -> p m j t", t=PACK, j=PACK)
-            nc.scalar.copy(dealt[:, m0:m1, :, :], raw[:].rearrange("p j (m t) -> p m j t", t=PACK))
+            copy(dealt[:, m0:m1, :, :], raw[:].rearrange("p j (m t) -> p m j t", t=PACK))
 
         def quantize(codes, scales, values):
             nc.vector.quantize_mx(out=codes.bitcast(FP8X4), scales=scales, in_=values)
 
-        def gather_words(name, table, offsets, h):
-            tile = held(name, [P, BANK], U32)
+        def gather_words(name, table, offsets, h, tag=None):
+            tile = held(name, [P, BANK], U32, tag)
             picked = table[:].bitcast(U32).indirect(offsets[:, h * LIST_COLS : (h + 1) * LIST_COLS])
             nc.vector.tensor_copy(tile[:], picked)
             return tile
 
-        round_w1(0, w1_raw0, 0)
+        def gather_scales2(h, tag):
+            tile = held("v2_rows%d" % h, [P, BANK], U8, tag)
+            nc.vector.tensor_copy(tile[:], tab2_plane[:].indirect(offs2_t[:, h * LIST_COLS : (h + 1) * LIST_COLS]))
+            for r in range(4):
+                nc.sync.dma_start(v2_scale[h][r : P : 32, :].bitcast(I32), tile[8 * r : P : 32, :].bitcast(I32))
+
+        round_w1(nc.scalar.copy, 0, w1_raw0, 0)
         v_words = [[None] * HALVES for a in range(PASSES)]
         for h in range(HALVES):
             v_words[0][h] = gather_words("v_words0%d" % h, tab_w0, offs_t, h)
-        quantize(w1_codes[0][:], w1_sc[0][:], w1_bf[0][:])
+        gather_scales2(0, "tab_w0")
         for h in range(HALVES):
             v_words[1][h] = gather_words("v_words1%d" % h, tab_w1, offs_t, h)
+        quantize(w1_codes[0][:], w1_sc[0][:], w1_bf[0][:])
 
         def pass_need(acc, t, h, a):
             cols = slice(t * P, (t + 1) * P)
@@ -166,18 +169,16 @@ def tile_list_sibling_placement_scores_kernel(
                 start=(a == 0), stop=(a == PASSES - 1),
             )
 
-        urge = [[held("urge%d%d" % (h, t), [P, BANK], F32) for t in range(PACK)] for h in range(HALVES)]
         h_rows = [held("h_rows%d" % h, [P, PACK, BANK], BF16) for h in range(HALVES)]
         h_woven = [held("h_woven%d" % h, [P, BANK * PACK], BF16) for h in range(HALVES)]
-        h_codes = [held("h_codes%d" % h, [P, BANK], U32) for h in range(HALVES)]
         h_sc = [held("h_sc%d" % h, [P, BANK], U8) for h in range(HALVES)]
 
         def sigmoid(acc, t, h):
-            nc.scalar.activation(urge[h][t][:], acc[:], ACT.Sigmoid, bias=bg_t[:, t : t + 1])
+            nc.scalar.activation(urge[h][:, t, :], acc[:], ACT.Sigmoid, bias=bg_t[:, t : t + 1])
 
         def product(acc, t, h):
             nc.vector.scalar_tensor_tensor(
-                h_rows[h][:, t, :], urge[h][t][:], cut_t[:, t : t + 1], acc[:], ALU.subtract, ALU.mult
+                h_rows[h][:, t, :], urge[h][:, t, :], cut_t[:, t : t + 1], acc[:], ALU.subtract, ALU.mult
             )
 
         def weave(copy, h):
@@ -186,69 +187,78 @@ def tile_list_sibling_placement_scores_kernel(
                 h_rows[h][:].rearrange("p t (c i) -> p c t i", i=PACK),
             )
 
-        gate0 = [bank(t) for t in range(PACK)]
-        need0 = [bank(PACK + t) for t in range(PACK)]
-        for t in range(PACK):
-            pass_gate(gate0[t], t, 0, 0)
-        for t in range(PACK):
-            pass_need(need0[t], t, 0, 0)
-        round_w1(1, w1_raw1[0], 0)
-        for t in range(PACK):
-            pass_gate(gate0[t], t, 0, 1)
-        sigmoid(gate0[0], 0, 0)
-        round_w1(1, w1_raw1[1], H // 2)
-        for t in range(1, PACK):
-            sigmoid(gate0[t], t, 0)
-
-        v2_scale = held("v2_scale", [P, S2], U8)
-        nc.vector.tensor_copy(v2_scale[:], tab2_plane[:].indirect(offs2_t[:]))
-
+        gate = [[bank(h * PACK + t) for t in range(PACK)] for h in range(HALVES)]
+        for a in range(PASSES):
+            for h in range(HALVES):
+                for t in range(PACK):
+                    pass_gate(gate[h][t], t, h, a)
+        round_w1(nc.scalar.copy, 1, w1_raw1[0], 0)
+        round_w1(nc.vector.tensor_copy, 1, w1_raw1[1], H // 2)
+        urge = [held("urge0", [P, PACK, BANK], F32, tag="w1_raw10"), held("urge1", [P, PACK, BANK], F32)]
+        for h in range(HALVES):
+            for t in range(PACK):
+                sigmoid(gate[h][t], t, h)
         for half in range(2):
             cols = slice(half * H // 2, (half + 1) * H // 2)
             quantize(w1_codes[1][:, cols], w1_sc[1][:, cols], w1_bf[1][:, half * 2 * H : (half + 1) * 2 * H])
-        for t in range(PACK):
-            pass_need(need0[t], t, 0, 1)
-        gate1 = [bank(t) for t in range(PACK)]
-        for t in range(PACK):
-            for a in range(PASSES):
-                pass_gate(gate1[t], t, 1, a)
-        for t in range(PACK):
-            product(need0[t], t, 0)
-        for t in range(PACK):
-            sigmoid(gate1[t], t, 1)
-        need1 = [bank(PACK + t) for t in range(PACK)]
-        for t in range(PACK):
-            for a in range(PASSES):
-                pass_need(need1[t], t, 1, a)
-        weave(nc.scalar.copy, 0)
-        for t in range(PACK):
-            product(need1[t], t, 1)
-        v2_words = [gather_words("v2_words0", tab2_w, offs2_t, 0)]
-        weave(nc.vector.tensor_copy, 1)
+        for h in range(HALVES):
+            for t in range(PACK):
+                need = bank(h * PACK + t)
+                for a in range(PASSES):
+                    pass_need(need, t, h, a)
+                product(need, t, h)
+            if h == 0:
+                weave(nc.scalar.copy, 0)
+        weave(nc.scalar.copy, 1)
+        v2_words = [
+            gather_words("v2_words0", tab2_w, offs2_t, 0, tag="urge1"),
+            gather_words("v2_words1", tab2_w, offs2_t, 1, tag="cut_t"),
+        ]
+        h_codes = [held("h_codes0", [P, BANK], U32), held("h_codes1", [P, BANK], U32, tag="tab2_w")]
         for h in range(HALVES):
             quantize(h_codes[h][:], h_sc[h][:], h_woven[h][:])
-        v2_words.append(gather_words("v2_words1", tab2_w, offs2_t, 1))
+        gather_scales2(1, "h_woven1")
 
         tiles_a_slice = BANK // P
-        for i in range(M_TILES):
+
+        def score(i):
             c0 = (i % tiles_a_slice) * P
-            scores = ring.tile([P, S], F32, name="scores")
+            scores = held("scores%d" % i, [P, S], F32)
             for h in range(HALVES):
                 acc = bank((HALVES * i + h) % 8)
                 nc.tensor.matmul_mx(
                     out=acc[:], lhsT=v2_words[i // tiles_a_slice][:, c0 : c0 + P].bitcast(FP8X4),
-                    lhsT_scale=v2_scale[:, i * P : (i + 1) * P],
+                    lhsT_scale=v2_scale[i // tiles_a_slice][:, c0 : c0 + P],
                     rhs=h_codes[h][:].bitcast(FP8X4), rhs_scale=h_sc[h][:], start=True, stop=True,
                 )
                 nc.scalar.copy(scores[:, h * BANK : (h + 1) * BANK], acc[:])
+            return scores
+
+        def pick(scores):
             first = ring.tile([P, NP], F32, name="first")
             second = ring.tile([P, NP], F32, name="second")
-            first_cap = ring.tile([P, NP], F32, name="first_cap")
-            lower = ring.tile([P, NP], F32, name="lower")
             nc.vector.tensor_copy(first[:], scores[:].indirect(pos1_t[:]))
             nc.vector.tensor_copy(second[:], scores[:].indirect(pos2_t[:]))
+            return first, second
+
+        def finish(i, first, second):
+            first_cap = ring.tile([P, NP], F32, name="first_cap")
             nc.scalar.activation(first_cap[:], first[:], ACT.Copy, scale=cap1_t[:, i : i + 1])
-            nc.vector.scalar_tensor_tensor(
-                lower[:], second[:], cap2_t[:, i : i + 1], first_cap[:], ALU.mult, ALU.min
-            )
-            nc.sync.dma_start(out[i * P : (i + 1) * P, :], lower[:])
+            lower = held("lower%d" % i, [P, NP], F32, tag="scores%d" % min(i + 1, M_TILES))
+            width = NP // 2 if i == M_TILES - 1 else NP
+            for c0 in range(0, NP, width):
+                cols = slice(c0, c0 + width)
+                nc.vector.scalar_tensor_tensor(
+                    lower[:, cols], second[:, cols], cap2_t[:, i : i + 1], first_cap[:, cols], ALU.mult, ALU.min
+                )
+                nc.sync.dma_start(out[i * P : (i + 1) * P, cols], lower[:, cols])
+
+        rows = [score(0), score(1)]
+        picked = pick(rows[0])
+        for i in range(1, M_TILES):
+            if i + 1 < M_TILES:
+                rows.append(score(i + 1))
+            ahead = pick(rows[i])
+            finish(i - 1, *picked)
+            picked = ahead
+        finish(M_TILES - 1, *picked)

from contextlib import ExitStack

import concourse.mybir as mybir

K, H, T, S, T3, S2, NP = 1024, 512, 2048, 1024, 4096, 1024, 512
FLOPS = 2 * (2 * K * H * S + H * S2 * S)

F32 = mybir.dt.float32
BF16 = mybir.dt.bfloat16
I32 = mybir.dt.int32
U32 = mybir.dt.uint32
U16 = mybir.dt.uint16
U8 = mybir.dt.uint8
FP8X4 = mybir.dt.float8_e4m3fn_x4
FP4X4 = mybir.dt.float4_e2m1fn_x4
ALU = mybir.AluOpType
ACT = mybir.ActivationFunctionType

P = 128
PACK = 4
PASSES = K // (P * PACK)
BANK = 512
HALVES = S // BANK
QUADS = 4
M_TILES = S2 // P
LIST_COLS = BANK // 16


def tile_list_sibling_placement_scores_kernel(
    tc, tab_words, tab_scales, tab2_words, tab2_scales, offs, offs2, pos1, pos2,
    w1, wg_words, wg_scales, bg, cut, cap1, cap2, out,
):
    nc = tc.nc
    with ExitStack() as ctx:
        lists = ctx.enter_context(tc.tile_pool(name="lists", bufs=1))
        keep = ctx.enter_context(tc.tile_pool(name="keep", bufs=1))
        ring = ctx.enter_context(tc.tile_pool(name="ring", bufs=3))
        psum = ctx.enter_context(tc.psum_pool(name="psum", bufs=1))

        def held(name, shape, dtype, tag=None):
            return keep.tile(shape, dtype, name=name, tag=tag or name, align_bytes=64)

        def load_list(name, src):
            tile = lists.tile(list(src.shape), U16, name=name)
            nc.sync.dma_start(tile[:], src)
            return tile

        def load_words(name, src):
            tile = held(name, [P, src.shape[1]], I32)
            nc.sync.dma_start(tile[:], src.rearrange("p t i -> p (t i)").bitcast(I32))
            return tile

        def load_w1(name, a, c0, c1):
            tile = held(name, [P, PACK, c1 - c0], F32)
            rows = w1[a * P * PACK : (a + 1) * P * PACK, c0:c1]
            nc.sync.dma_start(tile[:], rows.rearrange("(p j) c -> p j c", j=PACK))
            return tile

        def bank(b):
            return psum.tile([P, BANK], F32, name="bank%d" % b)

        tab_plane = held("tab_plane", [P, T], U8)
        wg_plane = held("wg_plane", [P, PASSES * H], U8)
        tab2_plane = held("tab2_plane", [P, T3], U8)
        v_scale1 = held("v_scale1", [P, S], U8)
        v2_scale = [held("v2_scale%d" % h, [P, BANK], U8) for h in range(HALVES)]
        for plane in (tab_plane, wg_plane, tab2_plane, v_scale1, *v2_scale):
            nc.vector.memset(plane[:].bitcast(I32), 0)


        warm = held("warm", [P, 2], F32)
        nc.vector.memset(warm[:, 0:1], 0.0)
        nc.scalar.activation(warm[:, 1:2], warm[:, 0:1], ACT.Sigmoid)

        offs_t = load_list("offs_t", offs)
        for r in range(4):
            nc.sync.dma_start(
                tab_plane[r : P : 16, :].bitcast(I32),
                tab_scales[:, r : 16 : 4, :].bitcast(I32).rearrange("a q n -> q a n"),
            )
        wg_raw = held("wg_raw", [P, PASSES, 2 * H // 4], I32)
        nc.sync.dma_start(wg_raw[:], wg_words.bitcast(I32).rearrange("a p n -> p a n"))
        tab_w0 = load_words("tab_w0", tab_words[0])
        for r in range(4):
            nc.sync.dma_start(
                wg_plane[r : P : 32, :].bitcast(I32).rearrange("q (a n) -> q a n", a=PASSES),
                wg_scales[:, r : 16 : 4, :].bitcast(I32).rearrange("a q n -> q a n"),
            )
        offs2_t = load_list("offs2_t", offs2)
        nc.sync.dma_start(tab2_plane[0 : P : 8, :].bitcast(I32), tab2_scales[0].bitcast(I32))
        w1_raw0 = load_w1("w1_raw0", 0, 0, H)
        tab_w1 = load_words("tab_w1", tab_words[1])

        v_scale0 = held("v_scale0", [P, S], U8)
        nc.vector.tensor_copy(v_scale0[:], tab_plane[:].indirect(offs_t[:]))
        nc.sync.dma_start(v_scale1[0:112, :].bitcast(I32), v_scale0[16:128, :].bitcast(I32))
        v_scale = [v_scale0, v_scale1]
        bg_t = held("bg_t", [P, PACK], F32)
        cut_t = held("cut_t", [P, PACK], F32)
        w1_raw1 = [load_w1("w1_raw1%d" % c, 1, c * H // 2, (c + 1) * H // 2) for c in range(2)]
        nc.sync.dma_start(bg_t[:], bg.rearrange("(p t) -> p t", t=PACK))
        nc.sync.dma_start(cut_t[:], cut.rearrange("(p t) -> p t", t=PACK))
        tab2_w = load_words("tab2_w", tab2_words[0])
        pos1_t = load_list("pos1_t", pos1)
        pos2_t = load_list("pos2_t", pos2)
        cap1_t = held("cap1_t", [P, M_TILES], F32)
        cap2_t = held("cap2_t", [P, M_TILES], F32)
        with nc.allow_non_contiguous_dma(reason="one capacity a partition and tile"):
            nc.sync.dma_start(cap1_t[:], cap1.rearrange("(i p) -> p i", p=P))
            nc.sync.dma_start(cap2_t[:], cap2.rearrange("(i p) -> p i", p=P))

        wg_codes = held("wg_codes", [P, PASSES * 2 * H], U8)
        wg_sc = held("wg_sc", [P, PASSES * H], U8)
        nc.vector.tensor_copy(
            wg_codes[:].bitcast(U16).rearrange("p (a t m) -> p a t m", a=PASSES, t=PACK),
            wg_raw[:].rearrange("p a n -> p (a n)").bitcast(U16).rearrange("p (a m t) -> p a t m", a=PASSES, t=PACK),
        )
        nc.vector.tensor_copy(
            wg_sc[:].rearrange("p (a t m) -> p a t m", a=PASSES, t=PACK),
            wg_plane[:].rearrange("p (a m t) -> p a t m", a=PASSES, t=PACK),
        )

        w1_bf = [held("w1_bf%d" % a, [P, H * PACK], BF16) for a in range(PASSES)]
        w1_codes = [held("w1_codes%d" % a, [P, H], U32) for a in range(PASSES)]
        w1_sc = [held("w1_sc%d" % a, [P, H], U8) for a in range(PASSES)]

        def round_w1(copy, a, raw, c0):
            m0, m1 = c0 // PACK, (c0 + raw.shape[2]) // PACK
            dealt = w1_bf[a][:].rearrange("p (t m j) -> p m j t", t=PACK, j=PACK)
            copy(dealt[:, m0:m1, :, :], raw[:].rearrange("p j (m t) -> p m j t", t=PACK))

        def quantize(codes, scales, values):
            nc.vector.quantize_mx(out=codes.bitcast(FP8X4), scales=scales, in_=values)

        def gather_words(name, table, offsets, h, tag=None):
            tile = held(name, [P, BANK], U32, tag)
            picked = table[:].bitcast(U32).indirect(offsets[:, h * LIST_COLS : (h + 1) * LIST_COLS])
            nc.vector.tensor_copy(tile[:], picked)
            return tile

        def gather_scales2(h, tag):
            tile = held("v2_rows%d" % h, [P, BANK], U8, tag)
            nc.vector.tensor_copy(tile[:], tab2_plane[:].indirect(offs2_t[:, h * LIST_COLS : (h + 1) * LIST_COLS]))
            for r in range(4):
                nc.sync.dma_start(v2_scale[h][r : P : 32, :].bitcast(I32), tile[8 * r : P : 32, :].bitcast(I32))

        round_w1(nc.scalar.copy, 0, w1_raw0, 0)
        v_words = [[None] * HALVES for a in range(PASSES)]
        for h in range(HALVES):
            v_words[0][h] = gather_words("v_words0%d" % h, tab_w0, offs_t, h)
        gather_scales2(0, "tab_w0")
        for h in range(HALVES):
            v_words[1][h] = gather_words("v_words1%d" % h, tab_w1, offs_t, h)
        quantize(w1_codes[0][:], w1_sc[0][:], w1_bf[0][:])

        def pass_need(acc, t, h, a):
            cols = slice(t * P, (t + 1) * P)
            nc.tensor.matmul_mx(
                out=acc[:], lhsT=w1_codes[a][:, cols].bitcast(FP8X4), lhsT_scale=w1_sc[a][:, cols],
                rhs=v_words[a][h][:].bitcast(FP8X4), rhs_scale=v_scale[a][:, h * BANK : (h + 1) * BANK],
                start=(a == 0), stop=(a == PASSES - 1),
            )

        def pass_gate(acc, t, h, a):
            c0 = a * H + t * P
            nc.tensor.matmul_mx(
                out=acc[:], lhsT=wg_codes[:, 2 * c0 : 2 * (c0 + P)].bitcast(FP4X4), lhsT_scale=wg_sc[:, c0 : c0 + P],
                rhs=v_words[a][h][:].bitcast(FP8X4), rhs_scale=v_scale[a][:, h * BANK : (h + 1) * BANK],
                start=(a == 0), stop=(a == PASSES - 1),
            )

        h_rows = [held("h_rows%d" % h, [P, PACK, BANK], BF16) for h in range(HALVES)]
        h_woven = [held("h_woven%d" % h, [P, BANK * PACK], BF16) for h in range(HALVES)]
        h_sc = [held("h_sc%d" % h, [P, BANK], U8) for h in range(HALVES)]

        def sigmoid(acc, t, h):
            nc.scalar.activation(urge[h][:, t, :], acc[:], ACT.Sigmoid, bias=bg_t[:, t : t + 1])

        def product(acc, t, h):
            nc.vector.scalar_tensor_tensor(
                h_rows[h][:, t, :], urge[h][:, t, :], cut_t[:, t : t + 1], acc[:], ALU.subtract, ALU.mult
            )

        def weave(copy, h):
            copy(
                h_woven[h][:].rearrange("p (c i t) -> p c t i", i=PACK, t=PACK),
                h_rows[h][:].rearrange("p t (c i) -> p c t i", i=PACK),
            )

        gate = [[bank(h * PACK + t) for t in range(PACK)] for h in range(HALVES)]
        for a in range(PASSES):
            for h in range(HALVES):
                for t in range(PACK):
                    pass_gate(gate[h][t], t, h, a)
        round_w1(nc.scalar.copy, 1, w1_raw1[0], 0)
        round_w1(nc.vector.tensor_copy, 1, w1_raw1[1], H // 2)
        urge = [held("urge0", [P, PACK, BANK], F32, tag="w1_raw10"), held("urge1", [P, PACK, BANK], F32)]
        for h in range(HALVES):
            for t in range(PACK):
                sigmoid(gate[h][t], t, h)
        for half in range(2):
            cols = slice(half * H // 2, (half + 1) * H // 2)
            quantize(w1_codes[1][:, cols], w1_sc[1][:, cols], w1_bf[1][:, half * 2 * H : (half + 1) * 2 * H])
        for h in range(HALVES):
            for t in range(PACK):
                need = bank(h * PACK + t)
                for a in range(PASSES):
                    pass_need(need, t, h, a)
                product(need, t, h)
            if h == 0:
                weave(nc.scalar.copy, 0)
        weave(nc.scalar.copy, 1)
        v2_words = [
            gather_words("v2_words0", tab2_w, offs2_t, 0, tag="urge1"),
            gather_words("v2_words1", tab2_w, offs2_t, 1, tag="cut_t"),
        ]
        h_codes = [held("h_codes0", [P, BANK], U32), held("h_codes1", [P, BANK], U32, tag="tab2_w")]
        for h in range(HALVES):
            quantize(h_codes[h][:], h_sc[h][:], h_woven[h][:])
        gather_scales2(1, "h_woven1")

        tiles_a_slice = BANK // P

        def score(i):
            c0 = (i % tiles_a_slice) * P
            scores = held("scores%d" % i, [P, S], F32)
            for h in range(HALVES):
                acc = bank((HALVES * i + h) % 8)
                nc.tensor.matmul_mx(
                    out=acc[:], lhsT=v2_words[i // tiles_a_slice][:, c0 : c0 + P].bitcast(FP8X4),
                    lhsT_scale=v2_scale[i // tiles_a_slice][:, c0 : c0 + P],
                    rhs=h_codes[h][:].bitcast(FP8X4), rhs_scale=h_sc[h][:], start=True, stop=True,
                )
                nc.scalar.copy(scores[:, h * BANK : (h + 1) * BANK], acc[:])
            return scores

        def pick(scores):
            first = ring.tile([P, NP], F32, name="first")
            second = ring.tile([P, NP], F32, name="second")
            nc.vector.tensor_copy(first[:], scores[:].indirect(pos1_t[:]))
            nc.vector.tensor_copy(second[:], scores[:].indirect(pos2_t[:]))
            return first, second

        def finish(i, first, second):
            first_cap = ring.tile([P, NP], F32, name="first_cap")
            nc.scalar.activation(first_cap[:], first[:], ACT.Copy, scale=cap1_t[:, i : i + 1])
            lower = held("lower%d" % i, [P, NP], F32, tag="scores%d" % min(i + 1, M_TILES))
            width = NP // 2 if i == M_TILES - 1 else NP
            for c0 in range(0, NP, width):
                cols = slice(c0, c0 + width)
                nc.vector.scalar_tensor_tensor(
                    lower[:, cols], second[:, cols], cap2_t[:, i : i + 1], first_cap[:, cols], ALU.mult, ALU.min
                )
                nc.sync.dma_start(out[i * P : (i + 1) * P, cols], lower[:, cols])

        rows = [score(0), score(1)]
        picked = pick(rows[0])
        for i in range(1, M_TILES):
            if i + 1 < M_TILES:
                rows.append(score(i + 1))
            ahead = pick(rows[i])
            finish(i - 1, *picked)
            picked = ahead
        finish(M_TILES - 1, *picked)
